import numpy as np
import ml_dtypes


def mxq(x, axis, fmt="e4m3"):
    dtype, down = {"e4m3": (ml_dtypes.float8_e4m3fn, 7), "e5m2": (ml_dtypes.float8_e5m2, 14)}[fmt]
    v = np.moveaxis(np.asarray(x, np.float32).astype(ml_dtypes.bfloat16).astype(np.float64), axis, -1)
    blocks = v.reshape(v.shape[:-1] + (-1, 32))
    amax = np.abs(blocks).max(-1, keepdims=True)
    byte = np.maximum(np.where(amax > 0, np.frexp(amax)[1] - 1 + 127, 0) - down, 1)
    scale = np.exp2(byte - 127.0)
    codes = (blocks / scale).astype(np.float32).astype(dtype).astype(np.float64)
    return np.moveaxis((codes * scale).reshape(v.shape), -1, axis)


WIDE = False


def mx_kscale(k):
    if not WIDE:
        return np.ones(k)
    levels = np.array([10, -10, 5, -5, 0])
    if k % 512:
        return np.exp2(np.random.permutation(np.resize(levels, k // 32))).repeat(32)
    a = np.empty((k // 512, 16))
    for p in range(k // 512):
        a[p, :8] = np.random.permutation(np.resize(levels, 8))
        for g in range(8):
            far = levels[np.abs(levels - a[p, g]) >= 10]
            a[p, g + 8] = far[np.random.randint(len(far))]
    return np.exp2(a.ravel()).repeat(32)


def f64(x):
    return np.asarray(x).astype(np.float64)


def striped(idx):
    return np.tile(idx.reshape(-1, 16).T, (8, 1)).astype(np.uint16)


def unstriped(offs):
    return offs[:16].T.reshape(-1).astype(np.int64)


K, T, E, C, N = 1024, 512, 8, 128, 256


def by_expert(wq, xq):
    return np.concatenate([wq[e].T @ xq[:, e * C:(e + 1) * C] for e in range(E)], axis=1)


def setup_inputs():
    n = np.random.standard_normal
    s = mx_kscale(K)[:, None]
    first = np.random.permutation(np.repeat(np.arange(E), T // E))
    second = (first + 1 + np.random.permutation(np.repeat(np.arange(E - 1), -(-T // (E - 1)))[:T])) % E
    while np.bincount(second, minlength=E).max() != T // E:
        load = np.bincount(second, minlength=E); hi, lo = int(load.argmax()), int(load.argmin())
        t = np.flatnonzero((second == hi) & (first != lo))[0]; second[t] = lo
    slot_token = np.empty(E * C, np.int64); pos = np.empty((2, T), np.int64); fill = np.zeros(E, np.int64)
    place = np.stack([np.random.permutation(C) for _ in range(E)])
    for r, deal in enumerate((first, second)):
        for t in np.random.permutation(T):
            e = deal[t]; j = e * C + place[e, fill[e]]; fill[e] += 1; slot_token[j] = t; pos[r, t] = j
    g = np.random.uniform(0.2, 0.8, T)
    return {
        "xT": (n((K, T)) * s).astype(np.float32),
        "w": (n((E, K, N)) / np.sqrt(K) / s[None]).astype(np.float32),
        "b": (0.3 * n((N, E))).astype(np.float32),
        "gate": np.stack([np.tile(g, (N, 1)), np.tile(1.0 - g, (N, 1))]).astype(np.float32),
        "offs": striped(slot_token),
        "pos1": striped(pos[0]),
        "pos2": striped(pos[1]),
    }


def reference(xT, w, b, gate, offs, pos1, pos2):
    idx = unstriped(offs)
    xq = mxq(f64(xT)[:, idx], 0, "e4m3")
    y = by_expert(mxq(f64(w), 1, "e4m3"), xq)
    y = y + np.repeat(f64(b), C, axis=1)
    return f64(gate[0]) * y[:, unstriped(pos1)] + f64(gate[1]) * y[:, unstriped(pos2)]

@@ -1,0 +1,196 @@
+from contextlib import ExitStack
+
+import concourse.mybir as mybir
+
+K, T, E, C, N = 1024, 512, 8, 128, 256
+FLOPS = 2 * K * N * E * C
+
+F32 = mybir.dt.float32
+BF16 = mybir.dt.bfloat16
+I32 = mybir.dt.int32
+U32 = mybir.dt.uint32
+U16 = mybir.dt.uint16
+U8 = mybir.dt.uint8
+FP8X4 = mybir.dt.float8_e4m3fn_x4
+MULT = mybir.AluOpType.mult
+ADD = mybir.AluOpType.add
+IDENTITY = mybir.ActivationFunctionType.Identity
+
+P = 128
+PACK = 4
+PASSES = K // (P * PACK)
+HALVES = N // P
+SLOTS = E * C
+CHUNKS = E * PASSES
+WINDOW = 1408
+RUN = 4
+
+X_SHARES = ((336, 176, 0), (0, 512, 0))
+UNITS = (
+    (0, 4, 0, 256, (0, 176, 80)),
+    (4, 8, 0, 256, (0, 176, 80)),
+    (8, 10, 0, 256, (0, 176, 80)),
+    (10, 12, 0, 256, (0, 176, 80)),
+    (12, 14, 0, 256, (64, 144, 48)),
+    (14, 15, 0, 256, (112, 144, 0)),
+    (15, 16, 0, 128, (128, 0, 0)),
+    (15, 16, 128, 256, (0, 128, 0)),
+)
+BLOCK = 4
+LATE_BANKS = 6
+
+
+def interleave(nc, grouped, raw, shares):
+    c0 = 0
+    n = grouped.shape[1]
+    for engine, width in zip(("vector", "scalar", "gpsimd"), shares):
+        if width == 0:
+            continue
+        c1 = c0 + width
+        if n > 1 and engine != "gpsimd":
+            pieces = [(
+                grouped[:, :, c0:c1, :].rearrange("p a (c i) j -> p a c j i", i=RUN),
+                raw[:, :, :, c0:c1].rearrange("p a j (c i) -> p a c j i", i=RUN),
+            )]
+        else:
+            pieces = [(
+                grouped[:, a, c0:c1, :].rearrange("p (c i) j -> p c j i", i=RUN),
+                raw[:, a, :, c0:c1].rearrange("p j (c i) -> p c j i", i=RUN),
+            ) for a in range(n)]
+        for dst, src in pieces:
+            if engine == "vector":
+                nc.vector.tensor_copy(out=dst, in_=src)
+            elif engine == "scalar":
+                nc.scalar.copy(out=dst, in_=src)
+            else:
+                nc.gpsimd.tensor_scalar(out=dst, in0=src, scalar1=1.0, scalar2=0.0, op0=MULT, op1=ADD)
+        c0 = c1
+
+
+def tile_routed_moe_kernel(tc, xT, w, b, gate, offs, pos1, pos2, out):
+    nc = tc.nc
+    with ExitStack() as ctx:
+        keep = ctx.enter_context(tc.tile_pool(name="keep", bufs=1))
+        psum = ctx.enter_context(tc.psum_pool(name="psum", bufs=1))
+
+        offs_t = keep.tile([P, SLOTS // 16], U16, name="offs_t")
+        nc.sync.dma_start(offs_t[:], offs)
+        x_view = xT.rearrange("(a p j) t -> a p j t", p=P, j=PACK)
+        x_raw = keep.tile([P, PASSES, PACK, T], F32, name="x_raw")
+        for a in range(PASSES):
+            nc.sync.dma_start(out=x_raw[:, a], in_=x_view[a])
+        b_sb = keep.tile([P, HALVES, E], F32, name="b_sb")
+        nc.scalar.dma_start(out=b_sb[:], in_=b.rearrange("(h p) e -> p h e", p=P))
+        w_view = w.rearrange("e (a p j) n -> e p a j n", p=P, j=PACK)
+        w_raw = keep.tile([P, CHUNKS, PACK, N], F32, name="w_raw")
+        for e in range(E):
+            q = e * PASSES
+            if e < E - 1:
+                nc.sync.dma_start(out=w_raw[:, q:q + PASSES], in_=w_view[e])
+            else:
+                for a in range(PASSES):
+                    nc.sync.dma_start(out=w_raw[:, q + a], in_=w_view[e, :, a])
+        pos_t = []
+        for r, lst in enumerate((pos1, pos2)):
+            t = keep.tile([P, T // 16], U16, name="pos_t%d" % r)
+            nc.sync.dma_start(t[:], lst)
+            pos_t.append(t)
+        gate_sb = {}
+        for h in range(HALVES):
+            for r in range(2):
+                t = keep.tile([P, T], F32, name="gate_sb%d_%d" % (r, h))
+                nc.sync.dma_start(out=t[:], in_=gate[r, h * P:(h + 1) * P, :])
+                gate_sb[r, h] = t
+
+        x_codes, x_scales = [], []
+        for a in range(PASSES):
+            cd = keep.tile([P, WINDOW], I32, name="x_codes%d" % a, align_bytes=64)
+            nc.vector.memset(cd[:, T:WINDOW], 0)
+            x_codes.append(cd)
+            sc = keep.tile([P, WINDOW], U8, name="x_scales%d" % a, align_bytes=64)
+            nc.gpsimd.memset(sc[:], 0)
+            x_scales.append(sc)
+        x_grouped = keep.tile([P, PASSES, T, PACK], BF16, name="x_grouped", align_bytes=64)
+        g_codes, g_scales = [], []
+        for a in range(PASSES):
+            interleave(nc, x_grouped[:, a:a + 1], x_raw[:, a:a + 1], X_SHARES[a])
+            nc.vector.quantize_mx(
+                out=x_codes[a][:, 0:T].bitcast(FP8X4),
+                scales=x_scales[a][:, 0:T],
+                in_=x_grouped[:, a].rearrange("p c j -> p (c j)"),
+            )
+            gc = keep.tile([P, SLOTS], U32, name="g_codes%d" % a, align_bytes=64)
+            nc.vector.tensor_copy(out=gc[:], in_=x_codes[a][:].bitcast(U32).indirect(offs_t[:]))
+            gs = keep.tile([P, SLOTS], U8, name="g_scales%d" % a, align_bytes=64)
+            nc.vector.tensor_copy(out=gs[:], in_=x_scales[a][:].indirect(offs_t[:]))
+            g_codes.append(gc)
+            g_scales.append(gs)
+
+        y = [keep.tile([P, SLOTS], F32, name="y%d" % h) for h in range(HALVES)]
+        w_grouped = keep.tile([P, CHUNKS, N, PACK], BF16, name="w_grouped", align_bytes=64)
+        w_codes = keep.tile([P, CHUNKS, N], U32, name="w_codes", align_bytes=64)
+        w_scales = keep.tile([P, CHUNKS, N], U8, name="w_scales", align_bytes=64)
+        early = [psum.tile([P, BLOCK, C], F32, name="early%d" % h) for h in range(HALVES)]
+        acc = {}
+        for e in range(BLOCK):
+            for h in range(HALVES):
+                acc[e, h] = early[h][:, e, :]
+
+        for q0, q1, c0, c1, shares in UNITS:
+            for q in range(q0, q1, PASSES):
+                q2 = min(q + PASSES, q1)
+                interleave(nc, w_grouped[:, q:q2, c0:c1], w_raw[:, q:q2, :, c0:c1], shares)
+            nc.vector.quantize_mx(
+                out=w_codes[:, q0:q1, c0:c1].rearrange("p q n -> p (q n)").bitcast(FP8X4),
+                scales=w_scales[:, q0:q1, c0:c1].rearrange("p q n -> p (q n)"),
+                in_=w_grouped[:, q0:q1, c0:c1].rearrange("p q c j -> p (q c j)"),
+            )
+            halves = range(c0 // P, c1 // P)
+            for q in range(q0, q1):
+                e, a = q // PASSES, q % PASSES
+                slots = slice(e * C, (e + 1) * C)
+                if e < BLOCK and a == 0:
+                    continue
+                for h in halves:
+                    if e >= BLOCK and a == 0:
+                        bank = ((e - BLOCK) * HALVES + h) % LATE_BANKS
+                        late = psum.tile([P, C], F32, name="late%d_%d" % (e, h), tag="late%d" % bank)
+                        acc[e, h] = late[:]
+                    feats = slice(h * P, (h + 1) * P)
+                    for a2 in (range(PASSES) if e < BLOCK else (a,)):
+                        nc.tensor.matmul_mx(
+                            out=acc[e, h],
+                            lhsT=w_codes[:, e * PASSES + a2, feats].bitcast(FP8X4),
+                            lhsT_scale=w_scales[:, e * PASSES + a2, feats],
+                            rhs=g_codes[a2][:, slots].bitcast(FP8X4),
+                            rhs_scale=g_scales[a2][:, slots],
+                            start=(a2 == 0),
+                            stop=(a2 == PASSES - 1),
+                        )
+                if a == PASSES - 1 and e >= BLOCK:
+                    for h in halves:
+                        nc.scalar.activation(
+                            out=y[h][:, slots],
+                            in_=acc[e, h],
+                            func=IDENTITY,
+                            bias=b_sb[:, h, e:e + 1],
+                            scale=1.0,
+                        )
+                if a == PASSES - 1 and e == BLOCK - 1:
+                    for h in range(HALVES):
+                        nc.vector.tensor_tensor(
+                            out=y[h][:, 0:BLOCK * C].rearrange("p (e c) -> p e c", c=C),
+                            in0=early[h][:],
+                            in1=b_sb[:, h, 0:BLOCK].unsqueeze(2).to_broadcast([P, BLOCK, C]),
+                            op=ADD,
+                        )
+
+        for h in range(HALVES):
+            part = []
+            for r in range(2):
+                t = keep.tile([P, T], F32, name="part%d_%d" % (r, h))
+                nc.vector.tensor_tensor(out=t[:], in0=y[h][:].indirect(pos_t[r][:]), in1=gate_sb[r, h][:], op=MULT)
+                part.append(t)
+            res = keep.tile([P, T], F32, name="res%d" % h)
+            nc.vector.tensor_tensor(out=res[:], in0=part[0][:], in1=part[1][:], op=ADD)
+            nc.sync.dma_start(out=out[h * P:(h + 1) * P, :], in_=res[:])

@@ -27,37 +27,32 @@ RUN = 4
 
 X_SHARES = ((336, 176, 0), (0, 512, 0))
 UNITS = (
-    (0, 4, 0, 256, (0, 176, 80)),
-    (4, 8, 0, 256, (0, 176, 80)),
-    (8, 10, 0, 256, (0, 176, 80)),
-    (10, 12, 0, 256, (0, 176, 80)),
-    (12, 14, 0, 256, (64, 144, 48)),
-    (14, 15, 0, 256, (112, 144, 0)),
+    (0, 4, 0, 256, (0, 192, 64)),
+    (4, 8, 0, 256, (0, 192, 64)),
+    (8, 10, 0, 256, (0, 192, 64)),
+    (10, 12, 0, 256, (0, 192, 64)),
+    (12, 14, 0, 256, (0, 192, 64)),
+    (14, 15, 0, 256, (0, 224, 32)),
     (15, 16, 0, 128, (128, 0, 0)),
     (15, 16, 128, 256, (0, 128, 0)),
 )
-BLOCK = 4
-LATE_BANKS = 6
+BLOCKS = ((0, 4, ("vector", "vector")), (4, 6, ("vector", "vector")), (6, 7, ("vector", "vector")), (7, 8, ("vector", "scalar")))
+PSUM_BANKS = 8
 
 
 def interleave(nc, grouped, raw, shares):
     c0 = 0
     n = grouped.shape[1]
-    for engine, width in zip(("vector", "scalar", "gpsimd"), shares):
-        if width == 0:
-            continue
+    for engine, width, step in zip(("vector", "scalar", "gpsimd"), shares, (n, PASSES, 1)):
         c1 = c0 + width
-        if n > 1 and engine != "gpsimd":
-            pieces = [(
-                grouped[:, :, c0:c1, :].rearrange("p a (c i) j -> p a c j i", i=RUN),
-                raw[:, :, :, c0:c1].rearrange("p a j (c i) -> p a c j i", i=RUN),
-            )]
-        else:
-            pieces = [(
-                grouped[:, a, c0:c1, :].rearrange("p (c i) j -> p c j i", i=RUN),
-                raw[:, a, :, c0:c1].rearrange("p j (c i) -> p c j i", i=RUN),
-            ) for a in range(n)]
-        for dst, src in pieces:
+        for a in (range(0, n, step) if width else ()):
+            a1 = min(a + step, n)
+            if a1 - a > 1:
+                dst = grouped[:, a:a1, c0:c1, :].rearrange("p a (c i) j -> p a c j i", i=RUN)
+                src = raw[:, a:a1, :, c0:c1].rearrange("p a j (c i) -> p a c j i", i=RUN)
+            else:
+                dst = grouped[:, a, c0:c1, :].rearrange("p (c i) j -> p c j i", i=RUN)
+                src = raw[:, a, :, c0:c1].rearrange("p j (c i) -> p c j i", i=RUN)
             if engine == "vector":
                 nc.vector.tensor_copy(out=dst, in_=src)
             elif engine == "scalar":
@@ -73,14 +68,14 @@ def tile_routed_moe_kernel(tc, xT, w, b, gate, offs, pos1, pos2, out):
         keep = ctx.enter_context(tc.tile_pool(name="keep", bufs=1))
         psum = ctx.enter_context(tc.psum_pool(name="psum", bufs=1))
 
-        offs_t = keep.tile([P, SLOTS // 16], U16, name="offs_t")
-        nc.sync.dma_start(offs_t[:], offs)
         x_view = xT.rearrange("(a p j) t -> a p j t", p=P, j=PACK)
         x_raw = keep.tile([P, PASSES, PACK, T], F32, name="x_raw")
-        for a in range(PASSES):
-            nc.sync.dma_start(out=x_raw[:, a], in_=x_view[a])
+        nc.sync.dma_start(out=x_raw[:, 0], in_=x_view[0])
+        offs_t = keep.tile([P, SLOTS // 16], U16, name="offs_t")
+        nc.sync.dma_start(offs_t[:], offs)
+        nc.sync.dma_start(out=x_raw[:, 1], in_=x_view[1])
         b_sb = keep.tile([P, HALVES, E], F32, name="b_sb")
-        nc.scalar.dma_start(out=b_sb[:], in_=b.rearrange("(h p) e -> p h e", p=P))
+        nc.sync.dma_start(out=b_sb[:], in_=b.rearrange("(h p) e -> p h e", p=P))
         w_view = w.rearrange("e (a p j) n -> e p a j n", p=P, j=PACK)
         w_raw = keep.tile([P, CHUNKS, PACK, N], F32, name="w_raw")
         for e in range(E):
@@ -130,36 +125,36 @@ def tile_routed_moe_kernel(tc, xT, w, b, gate, offs, pos1, pos2, out):
         w_grouped = keep.tile([P, CHUNKS, N, PACK], BF16, name="w_grouped", align_bytes=64)
         w_codes = keep.tile([P, CHUNKS, N], U32, name="w_codes", align_bytes=64)
         w_scales = keep.tile([P, CHUNKS, N], U8, name="w_scales", align_bytes=64)
-        early = [psum.tile([P, BLOCK, C], F32, name="early%d" % h) for h in range(HALVES)]
-        acc = {}
-        for e in range(BLOCK):
-            for h in range(HALVES):
-                acc[e, h] = early[h][:, e, :]
+        block_of = {}
+        for i, (e0, e1, engines) in enumerate(BLOCKS):
+            for e in range(e0, e1):
+                block_of[e] = (i, e0, e1, engines)
+        banks = {}
 
         for q0, q1, c0, c1, shares in UNITS:
-            for q in range(q0, q1, PASSES):
-                q2 = min(q + PASSES, q1)
-                interleave(nc, w_grouped[:, q:q2, c0:c1], w_raw[:, q:q2, :, c0:c1], shares)
+            interleave(nc, w_grouped[:, q0:q1, c0:c1], w_raw[:, q0:q1, :, c0:c1], shares)
             nc.vector.quantize_mx(
                 out=w_codes[:, q0:q1, c0:c1].rearrange("p q n -> p (q n)").bitcast(FP8X4),
                 scales=w_scales[:, q0:q1, c0:c1].rearrange("p q n -> p (q n)"),
                 in_=w_grouped[:, q0:q1, c0:c1].rearrange("p q c j -> p (q c j)"),
             )
             halves = range(c0 // P, c1 // P)
+            whole = q1 - q0 >= PASSES
             for q in range(q0, q1):
                 e, a = q // PASSES, q % PASSES
                 slots = slice(e * C, (e + 1) * C)
-                if e < BLOCK and a == 0:
+                if whole and a == 0:
                     continue
+                i, e0, e1, engines = block_of[e]
                 for h in halves:
-                    if e >= BLOCK and a == 0:
-                        bank = ((e - BLOCK) * HALVES + h) % LATE_BANKS
-                        late = psum.tile([P, C], F32, name="late%d_%d" % (e, h), tag="late%d" % bank)
-                        acc[e, h] = late[:]
+                    if (i, h) not in banks:
+                        banks[i, h] = psum.tile(
+                            [P, e1 - e0, C], F32, name="bank%d_%d" % (i, h), tag="bank%d" % ((i * HALVES + h) % PSUM_BANKS)
+                        )
                     feats = slice(h * P, (h + 1) * P)
-                    for a2 in (range(PASSES) if e < BLOCK else (a,)):
+                    for a2 in (range(PASSES) if whole else (a,)):
                         nc.tensor.matmul_mx(
-                            out=acc[e, h],
+                            out=banks[i, h][:, e - e0, :],
                             lhsT=w_codes[:, e * PASSES + a2, feats].bitcast(FP8X4),
                             lhsT_scale=w_scales[:, e * PASSES + a2, feats],
                             rhs=g_codes[a2][:, slots].bitcast(FP8X4),
@@ -167,21 +162,22 @@ def tile_routed_moe_kernel(tc, xT, w, b, gate, offs, pos1, pos2, out):
                             start=(a2 == 0),
                             stop=(a2 == PASSES - 1),
                         )
-                if a == PASSES - 1 and e >= BLOCK:
-                    for h in halves:
+                if a != PASSES - 1:
+                    continue
+                for h in halves:
+                    if engines[h] == "scalar":
                         nc.scalar.activation(
                             out=y[h][:, slots],
-                            in_=acc[e, h],
+                            in_=banks[i, h][:, e - e0, :],
                             func=IDENTITY,
                             bias=b_sb[:, h, e:e + 1],
                             scale=1.0,
                         )
-                if a == PASSES - 1 and e == BLOCK - 1:
-                    for h in range(HALVES):
+                    elif e == e1 - 1:
                         nc.vector.tensor_tensor(
-                            out=y[h][:, 0:BLOCK * C].rearrange("p (e c) -> p e c", c=C),
-                            in0=early[h][:],
-                            in1=b_sb[:, h, 0:BLOCK].unsqueeze(2).to_broadcast([P, BLOCK, C]),
+                            out=y[h][:, e0 * C:e1 * C].rearrange("p (e c) -> p e c", c=C),
+                            in0=banks[i, h][:],
+                            in1=b_sb[:, h, e0:e1].unsqueeze(2).to_broadcast([P, e1 - e0, C]),
                             op=ADD,
                         )
 

@@ -23,7 +23,7 @@ HALVES = N // P
 SLOTS = E * C
 CHUNKS = E * PASSES
 WINDOW = 1408
-RUN = 4
+RUN = 8
 
 X_SHARES = ((336, 176, 0), (0, 512, 0))
 UNITS = (

@@ -181,12 +181,22 @@ def tile_routed_moe_kernel(tc, xT, w, b, gate, offs, pos1, pos2, out):
                             op=ADD,
                         )
 
-        for h in range(HALVES):
-            part = []
-            for r in range(2):
-                t = keep.tile([P, T], F32, name="part%d_%d" % (r, h))
-                nc.vector.tensor_tensor(out=t[:], in0=y[h][:].indirect(pos_t[r][:]), in1=gate_sb[r, h][:], op=MULT)
-                part.append(t)
-            res = keep.tile([P, T], F32, name="res%d" % h)
-            nc.vector.tensor_tensor(out=res[:], in0=part[0][:], in1=part[1][:], op=ADD)
-            nc.sync.dma_start(out=out[h * P:(h + 1) * P, :], in_=res[:])
+        part = {}
+        res = [keep.tile([P, T], F32, name="res%d" % h) for h in range(HALVES)]
+
+        def fetch(h, r):
+            t = keep.tile([P, T], F32, name="part%d_%d" % (r, h))
+            nc.vector.tensor_tensor(out=t[:], in0=y[h][:].indirect(pos_t[r][:]), in1=gate_sb[r, h][:], op=MULT)
+            part[h, r] = t
+
+        def finish(h, t0, t1):
+            nc.vector.tensor_tensor(out=res[h][:, t0:t1], in0=part[h, 0][:, t0:t1], in1=part[h, 1][:, t0:t1], op=ADD)
+            nc.sync.dma_start(out=out[h * P:(h + 1) * P, t0:t1], in_=res[h][:, t0:t1])
+
+        fetch(0, 0)
+        fetch(0, 1)
+        fetch(1, 0)
+        finish(0, 0, T)
+        fetch(1, 1)
+        finish(1, 0, T // 2)
+        finish(1, T // 2, T)

@@ -1,6 +1,7 @@
 from contextlib import ExitStack
 
 import concourse.mybir as mybir
+from concourse.masks import make_identity
 
 K, T, E, C, N = 1024, 512, 8, 128, 256
 FLOPS = 2 * K * N * E * C
@@ -38,6 +39,7 @@ UNITS = (
 )
 BLOCKS = ((0, 4, ("vector", "vector")), (4, 6, ("vector", "vector")), (6, 7, ("vector", "vector")), (7, 8, ("vector", "scalar")))
 PSUM_BANKS = 8
+PE_SUM = 384
 
 
 def interleave(nc, grouped, raw, shares):
@@ -96,6 +98,9 @@ def tile_routed_moe_kernel(tc, xT, w, b, gate, offs, pos1, pos2, out):
                 t = keep.tile([P, T], F32, name="gate_sb%d_%d" % (r, h))
                 nc.sync.dma_start(out=t[:], in_=gate[r, h * P:(h + 1) * P, :])
                 gate_sb[r, h] = t
+
+        ident = keep.tile([P, P], F32, name="ident")
+        make_identity(nc, ident[:])
 
         x_codes, x_scales = [], []
         for a in range(PASSES):
@@ -195,8 +200,13 @@ def tile_routed_moe_kernel(tc, xT, w, b, gate, offs, pos1, pos2, out):
 
         fetch(0, 0)
         fetch(0, 1)
+        acc = psum.tile([P, PE_SUM], F32, name="acc", tag="bank0")
+        for r in range(2):
+            nc.tensor.matmul(acc[:], lhsT=ident[:], rhs=part[0, r][:, 0:PE_SUM], start=(r == 0), stop=(r == 1))
+        nc.scalar.copy(out=res[0][:, 0:PE_SUM], in_=acc[:])
+        nc.sync.dma_start(out=out[0:P, 0:PE_SUM], in_=res[0][:, 0:PE_SUM])
         fetch(1, 0)
-        finish(0, 0, T)
+        finish(0, PE_SUM, T)
         fetch(1, 1)
         finish(1, 0, T // 2)
         finish(1, T // 2, T)

@@ -39,7 +39,7 @@ UNITS = (
 )
 BLOCKS = ((0, 4, ("vector", "vector")), (4, 6, ("vector", "vector")), (6, 7, ("vector", "vector")), (7, 8, ("vector", "scalar")))
 PSUM_BANKS = 8
-PE_SUM = 384
+PE_SUM = 256
 
 
 def interleave(nc, grouped, raw, shares):
@@ -194,8 +194,10 @@ def tile_routed_moe_kernel(tc, xT, w, b, gate, offs, pos1, pos2, out):
             nc.vector.tensor_tensor(out=t[:], in0=y[h][:].indirect(pos_t[r][:]), in1=gate_sb[r, h][:], op=MULT)
             part[h, r] = t
 
-        def finish(h, t0, t1):
+        def add(h, t0, t1):
             nc.vector.tensor_tensor(out=res[h][:, t0:t1], in0=part[h, 0][:, t0:t1], in1=part[h, 1][:, t0:t1], op=ADD)
+
+        def store(h, t0, t1):
             nc.sync.dma_start(out=out[h * P:(h + 1) * P, t0:t1], in_=res[h][:, t0:t1])
 
         fetch(0, 0)
@@ -204,9 +206,11 @@ def tile_routed_moe_kernel(tc, xT, w, b, gate, offs, pos1, pos2, out):
         for r in range(2):
             nc.tensor.matmul(acc[:], lhsT=ident[:], rhs=part[0, r][:, 0:PE_SUM], start=(r == 0), stop=(r == 1))
         nc.scalar.copy(out=res[0][:, 0:PE_SUM], in_=acc[:])
-        nc.sync.dma_start(out=out[0:P, 0:PE_SUM], in_=res[0][:, 0:PE_SUM])
         fetch(1, 0)
-        finish(0, PE_SUM, T)
+        add(0, PE_SUM, T)
+        store(0, 0, T)
         fetch(1, 1)
-        finish(1, 0, T // 2)
-        finish(1, T // 2, T)
+        add(1, 0, T // 2)
+        store(1, 0, T // 2)
+        add(1, T // 2, T)
+        store(1, T // 2, T)

@@ -30,16 +30,17 @@ X_SHARES = ((336, 176, 0), (0, 512, 0))
 UNITS = (
     (0, 4, 0, 256, (0, 192, 64)),
     (4, 8, 0, 256, (0, 192, 64)),
-    (8, 10, 0, 256, (0, 192, 64)),
-    (10, 12, 0, 256, (0, 192, 64)),
-    (12, 14, 0, 256, (0, 192, 64)),
-    (14, 15, 0, 256, (0, 224, 32)),
+    (8, 10, 0, 256, (32, 224, 0)),
+    (10, 12, 0, 256, (32, 224, 0)),
+    (12, 14, 0, 256, (32, 224, 0)),
+    (14, 15, 0, 256, (32, 224, 0)),
     (15, 16, 0, 128, (128, 0, 0)),
     (15, 16, 128, 256, (0, 128, 0)),
 )
 BLOCKS = ((0, 4, ("vector", "vector")), (4, 6, ("vector", "vector")), (6, 7, ("vector", "vector")), (7, 8, ("vector", "scalar")))
 PSUM_BANKS = 8
 PE_SUM = 256
+PLANE = 4
 
 
 def interleave(nc, grouped, raw, shares):
@@ -102,29 +103,27 @@ def tile_routed_moe_kernel(tc, xT, w, b, gate, offs, pos1, pos2, out):
         ident = keep.tile([P, P], F32, name="ident")
         make_identity(nc, ident[:])
 
-        x_codes, x_scales = [], []
+        x_scales = keep.tile([P, WINDOW], U8, name="x_scales", align_bytes=64)
+        nc.gpsimd.memset(x_scales[:], 0)
+        g_scales = keep.tile([P, SLOTS], U8, name="g_scales", align_bytes=64)
+        x_codes = []
         for a in range(PASSES):
             cd = keep.tile([P, WINDOW], I32, name="x_codes%d" % a, align_bytes=64)
             nc.vector.memset(cd[:, T:WINDOW], 0)
             x_codes.append(cd)
-            sc = keep.tile([P, WINDOW], U8, name="x_scales%d" % a, align_bytes=64)
-            nc.gpsimd.memset(sc[:], 0)
-            x_scales.append(sc)
         x_grouped = keep.tile([P, PASSES, T, PACK], BF16, name="x_grouped", align_bytes=64)
-        g_codes, g_scales = [], []
+        g_codes = []
         for a in range(PASSES):
             interleave(nc, x_grouped[:, a:a + 1], x_raw[:, a:a + 1], X_SHARES[a])
             nc.vector.quantize_mx(
                 out=x_codes[a][:, 0:T].bitcast(FP8X4),
-                scales=x_scales[a][:, 0:T],
+                scales=x_scales[PLANE * a:P, 0:T],
                 in_=x_grouped[:, a].rearrange("p c j -> p (c j)"),
             )
             gc = keep.tile([P, SLOTS], U32, name="g_codes%d" % a, align_bytes=64)
             nc.vector.tensor_copy(out=gc[:], in_=x_codes[a][:].bitcast(U32).indirect(offs_t[:]))
-            gs = keep.tile([P, SLOTS], U8, name="g_scales%d" % a, align_bytes=64)
-            nc.vector.tensor_copy(out=gs[:], in_=x_scales[a][:].indirect(offs_t[:]))
             g_codes.append(gc)
-            g_scales.append(gs)
+        nc.vector.tensor_copy(out=g_scales[:], in_=x_scales[:].indirect(offs_t[:]))
 
         y = [keep.tile([P, SLOTS], F32, name="y%d" % h) for h in range(HALVES)]
         w_grouped = keep.tile([P, CHUNKS, N, PACK], BF16, name="w_grouped", align_bytes=64)
@@ -163,7 +162,7 @@ def tile_routed_moe_kernel(tc, xT, w, b, gate, offs, pos1, pos2, out):
                             lhsT=w_codes[:, e * PASSES + a2, feats].bitcast(FP8X4),
                             lhsT_scale=w_scales[:, e * PASSES + a2, feats],
                             rhs=g_codes[a2][:, slots].bitcast(FP8X4),
-                            rhs_scale=g_scales[a2][:, slots],
+                            rhs_scale=g_scales[PLANE * a2:P, slots],
                             start=(a2 == 0),
                             stop=(a2 == PASSES - 1),
                         )

@@ -29,16 +29,19 @@ RUN = 8
 X_SHARES = ((336, 176, 0), (0, 512, 0))
 UNITS = (
     (0, 4, 0, 256, (0, 192, 64)),
-    (4, 8, 0, 256, (0, 192, 64)),
-    (8, 10, 0, 256, (32, 224, 0)),
-    (10, 12, 0, 256, (32, 224, 0)),
-    (12, 14, 0, 256, (32, 224, 0)),
-    (14, 15, 0, 256, (32, 224, 0)),
-    (15, 16, 0, 128, (128, 0, 0)),
-    (15, 16, 128, 256, (0, 128, 0)),
+    (4, 6, 0, 256, (0, 192, 64)),
+    (6, 8, 0, 256, (0, 192, 64)),
+    (8, 10, 0, 256, (96, 160, 0)),
+    (10, 12, 0, 256, (96, 160, 0)),
+    (12, 13, 0, 256, (128, 128, 0)),
+    (13, 14, 0, 256, (128, 128, 0)),
+    (14, 15, 0, 256, (64, 192, 0)),
+    (15, 16, 0, 128, (64, 64, 0)),
+    (15, 16, 128, 256, (64, 64, 0)),
 )
-BLOCKS = ((0, 4, ("vector", "vector")), (4, 6, ("vector", "vector")), (6, 7, ("vector", "vector")), (7, 8, ("vector", "scalar")))
+BLOCKS = ((0, 4, ("vector", "vector")), (4, 6, ("vector", "vector")), (6, 8, ("vector", "vector")))
 PSUM_BANKS = 8
+BY_PASS = 6
 PE_SUM = 256
 PLANE = 4
 
@@ -83,7 +86,7 @@ def tile_routed_moe_kernel(tc, xT, w, b, gate, offs, pos1, pos2, out):
         w_raw = keep.tile([P, CHUNKS, PACK, N], F32, name="w_raw")
         for e in range(E):
             q = e * PASSES
-            if e < E - 1:
+            if e < BY_PASS:
                 nc.sync.dma_start(out=w_raw[:, q:q + PASSES], in_=w_view[e])
             else:
                 for a in range(PASSES):

@@ -24,7 +24,7 @@ HALVES = N // P
 SLOTS = E * C
 CHUNKS = E * PASSES
 WINDOW = 1408
-RUN = 8
+RUNS = {"vector": 4, "scalar": 8, "gpsimd": 8}
 
 X_SHARES = ((336, 176, 0), (0, 512, 0))
 UNITS = (
@@ -51,14 +51,15 @@ def interleave(nc, grouped, raw, shares):
     n = grouped.shape[1]
     for engine, width, step in zip(("vector", "scalar", "gpsimd"), shares, (n, PASSES, 1)):
         c1 = c0 + width
+        run = RUNS[engine]
         for a in (range(0, n, step) if width else ()):
             a1 = min(a + step, n)
             if a1 - a > 1:
-                dst = grouped[:, a:a1, c0:c1, :].rearrange("p a (c i) j -> p a c j i", i=RUN)
-                src = raw[:, a:a1, :, c0:c1].rearrange("p a j (c i) -> p a c j i", i=RUN)
+                dst = grouped[:, a:a1, c0:c1, :].rearrange("p a (c i) j -> p a c j i", i=run)
+                src = raw[:, a:a1, :, c0:c1].rearrange("p a j (c i) -> p a c j i", i=run)
             else:
-                dst = grouped[:, a, c0:c1, :].rearrange("p (c i) j -> p c j i", i=RUN)
-                src = raw[:, a, :, c0:c1].rearrange("p j (c i) -> p c j i", i=RUN)
+                dst = grouped[:, a, c0:c1, :].rearrange("p (c i) j -> p c j i", i=run)
+                src = raw[:, a, :, c0:c1].rearrange("p j (c i) -> p c j i", i=run)
             if engine == "vector":
                 nc.vector.tensor_copy(out=dst, in_=src)
             elif engine == "scalar":

from contextlib import ExitStack

import concourse.mybir as mybir
from concourse.masks import make_identity

K, T, E, C, N = 1024, 512, 8, 128, 256
FLOPS = 2 * K * N * E * C

F32 = mybir.dt.float32
BF16 = mybir.dt.bfloat16
I32 = mybir.dt.int32
U32 = mybir.dt.uint32
U16 = mybir.dt.uint16
U8 = mybir.dt.uint8
FP8X4 = mybir.dt.float8_e4m3fn_x4
MULT = mybir.AluOpType.mult
ADD = mybir.AluOpType.add
IDENTITY = mybir.ActivationFunctionType.Identity

P = 128
PACK = 4
PASSES = K // (P * PACK)
HALVES = N // P
SLOTS = E * C
CHUNKS = E * PASSES
WINDOW = 1408
RUNS = {"vector": 4, "scalar": 8, "gpsimd": 8}

X_SHARES = ((336, 176, 0), (0, 512, 0))
UNITS = (
    (0, 4, 0, 256, (0, 192, 64)),
    (4, 6, 0, 256, (0, 192, 64)),
    (6, 8, 0, 256, (0, 192, 64)),
    (8, 10, 0, 256, (96, 160, 0)),
    (10, 12, 0, 256, (96, 160, 0)),
    (12, 13, 0, 256, (128, 128, 0)),
    (13, 14, 0, 256, (128, 128, 0)),
    (14, 15, 0, 256, (64, 192, 0)),
    (15, 16, 0, 128, (64, 64, 0)),
    (15, 16, 128, 256, (64, 64, 0)),
)
BLOCKS = ((0, 4, ("vector", "vector")), (4, 6, ("vector", "vector")), (6, 8, ("vector", "vector")))
PSUM_BANKS = 8
BY_PASS = 6
PE_SUM = 256
PLANE = 4


def interleave(nc, grouped, raw, shares):
    c0 = 0
    n = grouped.shape[1]
    for engine, width, step in zip(("vector", "scalar", "gpsimd"), shares, (n, PASSES, 1)):
        c1 = c0 + width
        run = RUNS[engine]
        for a in (range(0, n, step) if width else ()):
            a1 = min(a + step, n)
            if a1 - a > 1:
                dst = grouped[:, a:a1, c0:c1, :].rearrange("p a (c i) j -> p a c j i", i=run)
                src = raw[:, a:a1, :, c0:c1].rearrange("p a j (c i) -> p a c j i", i=run)
            else:
                dst = grouped[:, a, c0:c1, :].rearrange("p (c i) j -> p c j i", i=run)
                src = raw[:, a, :, c0:c1].rearrange("p j (c i) -> p c j i", i=run)
            if engine == "vector":
                nc.vector.tensor_copy(out=dst, in_=src)
            elif engine == "scalar":
                nc.scalar.copy(out=dst, in_=src)
            else:
                nc.gpsimd.tensor_scalar(out=dst, in0=src, scalar1=1.0, scalar2=0.0, op0=MULT, op1=ADD)
        c0 = c1


def tile_routed_moe_kernel(tc, xT, w, b, gate, offs, pos1, pos2, out):
    nc = tc.nc
    with ExitStack() as ctx:
        keep = ctx.enter_context(tc.tile_pool(name="keep", bufs=1))
        psum = ctx.enter_context(tc.psum_pool(name="psum", bufs=1))

        x_view = xT.rearrange("(a p j) t -> a p j t", p=P, j=PACK)
        x_raw = keep.tile([P, PASSES, PACK, T], F32, name="x_raw")
        nc.sync.dma_start(out=x_raw[:, 0], in_=x_view[0])
        offs_t = keep.tile([P, SLOTS // 16], U16, name="offs_t")
        nc.sync.dma_start(offs_t[:], offs)
        nc.sync.dma_start(out=x_raw[:, 1], in_=x_view[1])
        b_sb = keep.tile([P, HALVES, E], F32, name="b_sb")
        nc.sync.dma_start(out=b_sb[:], in_=b.rearrange("(h p) e -> p h e", p=P))
        w_view = w.rearrange("e (a p j) n -> e p a j n", p=P, j=PACK)
        w_raw = keep.tile([P, CHUNKS, PACK, N], F32, name="w_raw")
        for e in range(E):
            q = e * PASSES
            if e < BY_PASS:
                nc.sync.dma_start(out=w_raw[:, q:q + PASSES], in_=w_view[e])
            else:
                for a in range(PASSES):
                    nc.sync.dma_start(out=w_raw[:, q + a], in_=w_view[e, :, a])
        pos_t = []
        for r, lst in enumerate((pos1, pos2)):
            t = keep.tile([P, T // 16], U16, name="pos_t%d" % r)
            nc.sync.dma_start(t[:], lst)
            pos_t.append(t)
        gate_sb = {}
        for h in range(HALVES):
            for r in range(2):
                t = keep.tile([P, T], F32, name="gate_sb%d_%d" % (r, h))
                nc.sync.dma_start(out=t[:], in_=gate[r, h * P:(h + 1) * P, :])
                gate_sb[r, h] = t

        ident = keep.tile([P, P], F32, name="ident")
        make_identity(nc, ident[:])

        x_scales = keep.tile([P, WINDOW], U8, name="x_scales", align_bytes=64)
        nc.gpsimd.memset(x_scales[:], 0)
        g_scales = keep.tile([P, SLOTS], U8, name="g_scales", align_bytes=64)
        x_codes = []
        for a in range(PASSES):
            cd = keep.tile([P, WINDOW], I32, name="x_codes%d" % a, align_bytes=64)
            nc.vector.memset(cd[:, T:WINDOW], 0)
            x_codes.append(cd)
        x_grouped = keep.tile([P, PASSES, T, PACK], BF16, name="x_grouped", align_bytes=64)
        g_codes = []
        for a in range(PASSES):
            interleave(nc, x_grouped[:, a:a + 1], x_raw[:, a:a + 1], X_SHARES[a])
            nc.vector.quantize_mx(
                out=x_codes[a][:, 0:T].bitcast(FP8X4),
                scales=x_scales[PLANE * a:P, 0:T],
                in_=x_grouped[:, a].rearrange("p c j -> p (c j)"),
            )
            gc = keep.tile([P, SLOTS], U32, name="g_codes%d" % a, align_bytes=64)
            nc.vector.tensor_copy(out=gc[:], in_=x_codes[a][:].bitcast(U32).indirect(offs_t[:]))
            g_codes.append(gc)
        nc.vector.tensor_copy(out=g_scales[:], in_=x_scales[:].indirect(offs_t[:]))

        y = [keep.tile([P, SLOTS], F32, name="y%d" % h) for h in range(HALVES)]
        w_grouped = keep.tile([P, CHUNKS, N, PACK], BF16, name="w_grouped", align_bytes=64)
        w_codes = keep.tile([P, CHUNKS, N], U32, name="w_codes", align_bytes=64)
        w_scales = keep.tile([P, CHUNKS, N], U8, name="w_scales", align_bytes=64)
        block_of = {}
        for i, (e0, e1, engines) in enumerate(BLOCKS):
            for e in range(e0, e1):
                block_of[e] = (i, e0, e1, engines)
        banks = {}

        for q0, q1, c0, c1, shares in UNITS:
            interleave(nc, w_grouped[:, q0:q1, c0:c1], w_raw[:, q0:q1, :, c0:c1], shares)
            nc.vector.quantize_mx(
                out=w_codes[:, q0:q1, c0:c1].rearrange("p q n -> p (q n)").bitcast(FP8X4),
                scales=w_scales[:, q0:q1, c0:c1].rearrange("p q n -> p (q n)"),
                in_=w_grouped[:, q0:q1, c0:c1].rearrange("p q c j -> p (q c j)"),
            )
            halves = range(c0 // P, c1 // P)
            whole = q1 - q0 >= PASSES
            for q in range(q0, q1):
                e, a = q // PASSES, q % PASSES
                slots = slice(e * C, (e + 1) * C)
                if whole and a == 0:
                    continue
                i, e0, e1, engines = block_of[e]
                for h in halves:
                    if (i, h) not in banks:
                        banks[i, h] = psum.tile(
                            [P, e1 - e0, C], F32, name="bank%d_%d" % (i, h), tag="bank%d" % ((i * HALVES + h) % PSUM_BANKS)
                        )
                    feats = slice(h * P, (h + 1) * P)
                    for a2 in (range(PASSES) if whole else (a,)):
                        nc.tensor.matmul_mx(
                            out=banks[i, h][:, e - e0, :],
                            lhsT=w_codes[:, e * PASSES + a2, feats].bitcast(FP8X4),
                            lhsT_scale=w_scales[:, e * PASSES + a2, feats],
                            rhs=g_codes[a2][:, slots].bitcast(FP8X4),
                            rhs_scale=g_scales[PLANE * a2:P, slots],
                            start=(a2 == 0),
                            stop=(a2 == PASSES - 1),
                        )
                if a != PASSES - 1:
                    continue
                for h in halves:
                    if engines[h] == "scalar":
                        nc.scalar.activation(
                            out=y[h][:, slots],
                            in_=banks[i, h][:, e - e0, :],
                            func=IDENTITY,
                            bias=b_sb[:, h, e:e + 1],
                            scale=1.0,
                        )
                    elif e == e1 - 1:
                        nc.vector.tensor_tensor(
                            out=y[h][:, e0 * C:e1 * C].rearrange("p (e c) -> p e c", c=C),
                            in0=banks[i, h][:],
                            in1=b_sb[:, h, e0:e1].unsqueeze(2).to_broadcast([P, e1 - e0, C]),
                            op=ADD,
                        )

        part = {}
        res = [keep.tile([P, T], F32, name="res%d" % h) for h in range(HALVES)]

        def fetch(h, r):
            t = keep.tile([P, T], F32, name="part%d_%d" % (r, h))
            nc.vector.tensor_tensor(out=t[:], in0=y[h][:].indirect(pos_t[r][:]), in1=gate_sb[r, h][:], op=MULT)
            part[h, r] = t

        def add(h, t0, t1):
            nc.vector.tensor_tensor(out=res[h][:, t0:t1], in0=part[h, 0][:, t0:t1], in1=part[h, 1][:, t0:t1], op=ADD)

        def store(h, t0, t1):
            nc.sync.dma_start(out=out[h * P:(h + 1) * P, t0:t1], in_=res[h][:, t0:t1])

        fetch(0, 0)
        fetch(0, 1)
        acc = psum.tile([P, PE_SUM], F32, name="acc", tag="bank0")
        for r in range(2):
            nc.tensor.matmul(acc[:], lhsT=ident[:], rhs=part[0, r][:, 0:PE_SUM], start=(r == 0), stop=(r == 1))
        nc.scalar.copy(out=res[0][:, 0:PE_SUM], in_=acc[:])
        fetch(1, 0)
        add(0, PE_SUM, T)
        store(0, 0, T)
        fetch(1, 1)
        add(1, 0, T // 2)
        store(1, 0, T // 2)
        add(1, T // 2, T)
        store(1, T // 2, T)
